import numpy as np
import ml_dtypes


def mxq(x, axis, fmt="e4m3"):
    dtype, down = {"e4m3": (ml_dtypes.float8_e4m3fn, 7), "e5m2": (ml_dtypes.float8_e5m2, 14)}[fmt]
    v = np.moveaxis(np.asarray(x, np.float32).astype(ml_dtypes.bfloat16).astype(np.float64), axis, -1)
    blocks = v.reshape(v.shape[:-1] + (-1, 32))
    amax = np.abs(blocks).max(-1, keepdims=True)
    byte = np.maximum(np.where(amax > 0, np.frexp(amax)[1] - 1 + 127, 0) - down, 1)
    scale = np.exp2(byte - 127.0)
    codes = (blocks / scale).astype(np.float32).astype(dtype).astype(np.float64)
    return np.moveaxis((codes * scale).reshape(v.shape), -1, axis)


WIDE = False


def mx_kscale(k):
    if not WIDE:
        return np.ones(k)
    levels = np.array([10, -10, 5, -5, 0])
    if k % 512:
        return np.exp2(np.random.permutation(np.resize(levels, k // 32))).repeat(32)
    a = np.empty((k // 512, 16))
    for p in range(k // 512):
        a[p, :8] = np.random.permutation(np.resize(levels, 8))
        for g in range(8):
            far = levels[np.abs(levels - a[p, g]) >= 10]
            a[p, g + 8] = far[np.random.randint(len(far))]
    return np.exp2(a.ravel()).repeat(32)


def f64(x):
    return np.asarray(x).astype(np.float64)


def striped(idx):
    return np.tile(idx.reshape(-1, 16).T, (8, 1)).astype(np.uint16)


def unstriped(offs):
    return offs[:16].T.reshape(-1).astype(np.int64)


def striped8(idx):
    return np.concatenate([x.reshape(-1, 16).T for x in idx]).astype(np.uint16)


def runs(offs, k):
    lists = np.stack([offs[16 * r : 16 * r + 16].T.reshape(-1) for r in range(8)]).astype(np.int64)
    return lists[np.arange(k) % 512 // 64]


def pack_weight(w):
    k, n = w.shape
    w = f64(np.asarray(w, np.float32).astype(ml_dtypes.bfloat16)).reshape(k // 32, 32, n)
    amax = np.abs(w).max(1)
    byte = np.clip(np.where(amax > 0, np.frexp(amax)[1] - 1 + 127 - 7, 1), 1, 254)
    scaled = (w * np.exp2(127.0 - byte)[:, None, :]).reshape(k, n).astype(np.float32)
    words = np.ascontiguousarray(scaled.reshape(k // 512, 128, 4, n).transpose(0, 1, 3, 2)).astype(ml_dtypes.float8_e4m3fn).view(np.uint8)
    return words, np.ascontiguousarray(byte.astype(np.uint8).reshape(k // 512, 16, n))


def unpack_weight(words, scales):
    g, p, n, _ = words.shape
    vals = np.ascontiguousarray(words).view(ml_dtypes.float8_e4m3fn).astype(np.float64) * np.repeat(np.exp2(scales.astype(np.float64) - 127.0), 8, axis=1)[..., None]
    return vals.transpose(0, 1, 3, 2).reshape(g * 512, n)

def planes(y):
    n, m = y.shape
    v = y.astype(np.float32).astype(ml_dtypes.bfloat16).astype(np.float64).reshape(n // 32, 32, m)
    top = np.abs(v).max(1)
    byte = np.clip(np.where(top > 0, np.frexp(top)[1] - 1 + 127 - 7, 1), 1, 254)
    codes = (v * np.exp2(127.0 - byte)[:, None, :]).reshape(n, m).astype(np.float32).astype(ml_dtypes.float8_e4m3fn).view(np.uint8)
    words = codes.reshape(n // 512, 128, 4, m).transpose(0, 1, 3, 2)
    return np.ascontiguousarray(words), np.ascontiguousarray(byte.astype(np.uint8).reshape(n // 512, 16, m))


K, T, S, N, H, W = 512, 2048, 256, 512, 512, 128


def setup_inputs():
    n = np.random.standard_normal
    s = mx_kscale(K)[:, None]
    u = mx_kscale(H)
    packed_xT = pack_weight(n((K, T)) * s)
    packed_w1 = pack_weight(n((K, H)) / np.sqrt(K) / s)
    packed_w2 = pack_weight(n((H, N)) / np.sqrt(2 * H) / u[:, None])
    packed_w3 = pack_weight(n((K, N)) / np.sqrt(2 * K) / s)
    perm = np.random.permutation(S)
    return {
        "x_words": packed_xT[0],
        "x_scales": packed_xT[1],
        "w1_words": packed_w1[0],
        "w1_scales": packed_w1[1],
        "gn": (np.random.uniform(0.5, 1.5, (H, 1)) * u[:, None]).astype(np.float32),
        "w2_words": packed_w2[0],
        "w2_scales": packed_w2[1],
        "w3_words": packed_w3[0],
        "w3_scales": packed_w3[1],
        "offs": striped(np.random.permutation(T)[:S]),
        "n1": striped(perm[:W]),
        "n2": striped(perm[W:]),
        "two": striped(np.random.permutation(T)[:S]),
        "n3": striped8(np.stack([np.random.permutation(S) for _ in range(8)])),
    }


def reference(x_words, x_scales, w1_words, w1_scales, gn, w2_words, w2_scales, w3_words, w3_scales, offs, n1, n2, two, n3):
    xq = unpack_weight(x_words, x_scales)[:, unstriped(offs)]
    y = unpack_weight(w1_words, w1_scales).T @ xq
    pa = y[:, unstriped(n1)]
    pb = y[:, unstriped(n2)]
    rb = np.maximum(0.5 * pa, pb)
    ra = pb - pa
    ds = np.zeros((H, S))
    ds[:, unstriped(n1)] = ra
    dt = ds.copy()
    dt[:, unstriped(n2)] = rb
    z = f64(gn) * dt
    x_two = unpack_weight(x_words, x_scales)[:, unstriped(two)]
    h = unpack_weight(w2_words, w2_scales).T @ mxq(z, 0, "e4m3") + unpack_weight(w3_words, w3_scales).T @ x_two
    pa2 = h[np.arange(N)[:, None], runs(n3, N)]
    out_0 = (2.0 * (h * pa2)) / ((h) ** 2 + (pa2) ** 2 + 0.5)
    return (out_0,) + planes(out_0)

@@ -1,0 +1,265 @@
+from contextlib import ExitStack
+
+import concourse.mybir as mybir
+
+K, T, S, N, H, W = 512, 2048, 256, 512, 512, 128
+FLOPS = 3 * 2 * 512 * 512 * 256
+
+F32 = mybir.dt.float32
+BF16 = mybir.dt.bfloat16
+I32 = mybir.dt.int32
+U32 = mybir.dt.uint32
+U16 = mybir.dt.uint16
+U8 = mybir.dt.uint8
+FP8X4 = mybir.dt.float8_e4m3fn_x4
+ALU = mybir.AluOpType
+ACT = mybir.ActivationFunctionType
+
+P = 128
+PACK = 4
+QUADS = 4
+
+
+def words_of(dram):
+    return dram[0].rearrange("p n t -> p (n t)").bitcast(I32)
+
+
+def load_scale_rows(queue, tile, first, dram):
+    for q in range(QUADS):
+        queue.dma_start(
+            out=tile[32 * q + first : 32 * q + first + 4, :].bitcast(I32),
+            in_=dram[0, 4 * q : 4 * q + 4, :].bitcast(I32),
+        )
+
+
+def dealt(ap):
+    return ap.rearrange("p (t m) -> p m t", t=PACK)
+
+
+def plain(ap):
+    return ap.rearrange("p (m t) -> p m t", t=PACK)
+
+
+def tile_picked_mixinliftharm_none_po_kernel(
+    tc, x_words, x_scales, w1_words, w1_scales, gn, w2_words, w2_scales, w3_words, w3_scales,
+    offs, n1, n2, two, n3, out_0, out_1, out_2,
+):
+    nc = tc.nc
+    with ExitStack() as ctx:
+        keep = ctx.enter_context(tc.tile_pool(name="keep", bufs=1))
+        psum = ctx.enter_context(tc.psum_pool(name="psum", bufs=1))
+
+        def sb(shape, dtype, name):
+            return keep.tile(shape, dtype, name=name, align_bytes=64)
+
+        offs_t = sb([P, S // 16], U16, "offs_t")
+        n1_t = sb([P, W // 16], U16, "n1_t")
+        n2_t = sb([P, W // 16], U16, "n2_t")
+        two_t = sb([P, S // 16], U16, "two_t")
+        n3_t = sb([P, S // 16], U16, "n3_t")
+        xw = sb([P, T], U32, "xw")
+        xs = sb([P, T], U8, "xs")
+        w1w = sb([P, H], U32, "w1w")
+        w2w = sb([P, N], U32, "w2w")
+        w3w = sb([P, N], U32, "w3w")
+        w1s = sb([P, H], U8, "w1s")
+        w23s = sb([P, N], U8, "w23s")
+        gn_t = sb([P, PACK], F32, "gn_t")
+
+        nc.vector.memset(xs[:].bitcast(I32), 0)
+        nc.vector.memset(w1s[:].bitcast(I32), 0)
+        nc.gpsimd.memset(w23s[:].bitcast(I32), 0)
+
+        nc.sync.dma_start(offs_t[:], offs)
+        nc.scalar.dma_start(out=w1w[:].bitcast(I32), in_=words_of(w1_words))
+        nc.scalar.dma_start(out=xw[:].bitcast(I32), in_=words_of(x_words))
+        load_scale_rows(nc.sync, xs, 0, x_scales)
+        nc.sync.dma_start(n1_t[:], n1)
+        nc.sync.dma_start(n2_t[:], n2)
+        load_scale_rows(nc.scalar, w1s, 0, w1_scales)
+        nc.sync.dma_start(two_t[:], two)
+        nc.sync.dma_start(out=gn_t[:], in_=gn.rearrange("(p t) o -> p (t o)", t=PACK))
+        nc.sync.dma_start(out=w3w[:].bitcast(I32), in_=words_of(w3_words))
+        nc.sync.dma_start(out=w2w[:].bitcast(I32), in_=words_of(w2_words))
+        load_scale_rows(nc.sync, w23s, 0, w3_scales)
+        load_scale_rows(nc.sync, w23s, 4, w2_scales)
+        nc.sync.dma_start(n3_t[:], n3)
+
+        w1w_d = sb([P, H], U32, "w1w_d")
+        w1s_d = sb([P, H], U8, "w1s_d")
+        nc.vector.tensor_copy(out=dealt(w1w_d[:]), in_=plain(w1w[:]))
+        xq_s = sb([P, S], U8, "xq_s")
+        nc.vector.tensor_copy(out=xq_s[:], in_=xs[:].indirect(offs_t[:]))
+        xq_w = sb([P, S], U32, "xq_w")
+        nc.vector.tensor_copy(out=xq_w[:], in_=xw[:].indirect(offs_t[:]))
+        nc.vector.tensor_copy(out=dealt(w1s_d[:]), in_=plain(w1s[:]))
+
+        y = []
+        for t in range(PACK):
+            cols = slice(t * P, (t + 1) * P)
+            y_ps = psum.tile([P, S], F32, name=f"y_ps{t}")
+            nc.tensor.matmul_mx(
+                out=y_ps[:], lhsT=w1w_d[:, cols].bitcast(FP8X4), lhsT_scale=w1s_d[:, cols],
+                rhs=xq_w[:].bitcast(FP8X4), rhs_scale=xq_s[:], start=True, stop=True,
+            )
+            y_t = sb([P, S], F32, f"y{t}")
+            nc.vector.tensor_copy(out=y_t[:], in_=y_ps[:])
+            y.append(y_t)
+
+        pa = [sb([P, W], F32, f"pa{t}") for t in range(PACK)]
+        pb = [sb([P, W], F32, f"pb{t}") for t in range(PACK)]
+        ra = [sb([P, W], F32, f"ra{t}") for t in range(PACK)]
+        rb = [sb([P, W], F32, f"rb{t}") for t in range(PACK)]
+        dt = [sb([P, S], F32, f"dt{t}") for t in range(PACK)]
+        z = sb([P, S, PACK], BF16, "z")
+
+        def fetch_a(t):
+            nc.scalar.activation(out=pa[t][:], in_=y[t][:].indirect(n1_t[:]), func=ACT.Copy)
+
+        def fetch_b(t):
+            nc.scalar.activation(out=pb[t][:], in_=y[t][:].indirect(n2_t[:]), func=ACT.Copy)
+            nc.vector.tensor_tensor(out=ra[t][:], in0=pb[t][:], in1=pa[t][:], op=ALU.subtract)
+            nc.vector.scalar_tensor_tensor(
+                out=rb[t][:], in0=pa[t][:], scalar=0.5, in1=pb[t][:], op0=ALU.mult, op1=ALU.max
+            )
+
+        def put_a(t):
+            nc.scalar.activation(out=dt[t][:].indirect(n1_t[:]), in_=ra[t][:], func=ACT.Copy)
+
+        def put_b(t):
+            nc.scalar.activation(out=dt[t][:].indirect(n2_t[:]), in_=rb[t][:], func=ACT.Copy)
+            nc.vector.tensor_scalar(
+                out=z[:, :, t], in0=dt[t][:], scalar1=gn_t[:, t : t + 1], scalar2=None, op0=ALU.mult
+            )
+
+        fetch_a(0)
+        fetch_b(0)
+        fetch_a(1)
+        fetch_b(1)
+
+        w3w_d = sb([P, N], U32, "w3w_d")
+        w2w_d = sb([P, N], U32, "w2w_d")
+        w23s_d = sb([P, N], U8, "w23s_d")
+        x2_w = sb([P, S], U32, "x2_w")
+        x2_s = sb([P, S], U8, "x2_s")
+
+        put_a(0)
+        fetch_a(2)
+        put_b(0)
+        fetch_b(2)
+        nc.vector.tensor_copy(out=x2_w[:], in_=xw[:].indirect(two_t[:]))
+        nc.vector.tensor_copy(out=x2_s[:], in_=xs[:].indirect(two_t[:]))
+        put_a(1)
+        fetch_a(3)
+        put_b(1)
+        fetch_b(3)
+        nc.vector.tensor_copy(out=dealt(w3w_d[:]), in_=plain(w3w[:]))
+        nc.gpsimd.tensor_copy(out=dealt(w23s_d[:]), in_=plain(w23s[:]))
+        nc.vector.tensor_copy(out=dealt(w2w_d[:]), in_=plain(w2w[:]))
+        h_ps = [psum.tile([P, S], F32, name=f"h_ps{t}") for t in range(PACK)]
+        for t in range(PACK):
+            cols = slice(t * P, (t + 1) * P)
+            nc.tensor.matmul_mx(
+                out=h_ps[t][:], lhsT=w3w_d[:, cols].bitcast(FP8X4), lhsT_scale=w23s_d[:, cols],
+                rhs=x2_w[:].bitcast(FP8X4), rhs_scale=x2_s[:], start=True, stop=False,
+            )
+        put_a(2)
+        put_a(3)
+        put_b(2)
+        put_b(3)
+
+        zq_w = sb([P, S], U32, "zq_w")
+        zq_s = sb([P, S], U8, "zq_s")
+        nc.vector.quantize_mx(
+            out=zq_w[:].bitcast(FP8X4), scales=zq_s[:], in_=z[:].rearrange("p j t -> p (j t)")
+        )
+        for t in range(PACK):
+            cols = slice(t * P, (t + 1) * P)
+            nc.tensor.matmul_mx(
+                out=h_ps[t][:], lhsT=w2w_d[:, cols].bitcast(FP8X4), lhsT_scale=w23s_d[4:P, cols],
+                rhs=zq_w[:].bitcast(FP8X4), rhs_scale=zq_s[:], start=False, stop=True,
+            )
+
+        h = [sb([P, S], F32, f"h{t}") for t in range(PACK)]
+        pa2 = [sb([P, S], F32, f"pa2_{t}") for t in range(PACK)]
+        hh = [sb([P, S], F32, f"hh{t}") for t in range(PACK)]
+        pp = [sb([P, S], F32, f"pp{t}") for t in range(PACK)]
+        den = [sb([P, S], F32, f"den{t}") for t in range(PACK)]
+        rs = [sb([P, S], F32, f"rs{t}") for t in range(PACK)]
+        num = [sb([P, S], F32, f"num{t}") for t in range(PACK)]
+        half = [sb([P, S], F32, f"half{t}") for t in range(PACK)]
+        res = [sb([P, 2, S], F32, f"res{u}") for u in range(2)]
+        res_bf = sb([P, S, PACK], BF16, "res_bf")
+        out_rows = out_0.rearrange("(p t) j -> p t j", t=PACK)
+
+        def leave(t, on_scalar):
+            if on_scalar:
+                nc.scalar.copy(out=h[t][:], in_=h_ps[t][:])
+            else:
+                nc.vector.tensor_copy(out=h[t][:], in_=h_ps[t][:])
+
+        def fetch(t):
+            for u in range(2):
+                nc.scalar.activation(
+                    out=pa2[t][:, u * W : (u + 1) * W],
+                    in_=h[t][:].indirect(n3_t[:, u * 8 : (u + 1) * 8]), func=ACT.Copy,
+                )
+
+        def square_h(t, on_scalar):
+            if on_scalar:
+                nc.scalar.activation(out=hh[t][:], in_=h[t][:], func=ACT.Square)
+            else:
+                nc.vector.tensor_tensor(out=hh[t][:], in0=h[t][:], in1=h[t][:], op=ALU.mult)
+
+        def sums(t):
+            nc.scalar.activation(out=pp[t][:], in_=pa2[t][:], func=ACT.Square)
+            nc.vector.scalar_tensor_tensor(
+                out=num[t][:], in0=h[t][:], scalar=2.0, in1=pa2[t][:], op0=ALU.mult, op1=ALU.mult
+            )
+            nc.vector.scalar_tensor_tensor(
+                out=den[t][:], in0=hh[t][:], scalar=0.5, in1=pp[t][:], op0=ALU.add, op1=ALU.add
+            )
+
+        def finish(t):
+            nc.scalar.activation(out=rs[t][:], in_=den[t][:], func=ACT.Abs_reciprocal_sqrt)
+            nc.vector.tensor_tensor(out=half[t][:], in0=num[t][:], in1=rs[t][:], op=ALU.mult)
+            nc.vector.tensor_tensor(out=res[t // 2][:, t % 2, :], in0=half[t][:], in1=rs[t][:], op=ALU.mult)
+            nc.sync.dma_start(out=out_rows[:, t, :], in_=res[t // 2][:, t % 2, :])
+            if t % 2 == 1:
+                nc.vector.tensor_copy(
+                    out=res_bf[:, :, t - 1 : t + 1], in_=res[t // 2][:].rearrange("p t j -> p j t")
+                )
+
+        leave(0, False)
+        leave(1, True)
+        leave(2, False)
+        leave(3, False)
+        fetch(0)
+        square_h(0, False)
+        square_h(1, False)
+        sums(0)
+        fetch(1)
+        finish(0)
+        sums(1)
+        fetch(2)
+        square_h(2, True)
+        finish(1)
+        sums(2)
+        fetch(3)
+        square_h(3, True)
+        sums(3)
+        finish(2)
+        finish(3)
+
+        oq_w = sb([P, S], U32, "oq_w")
+        oq_s = sb([P, S], U8, "oq_s")
+        nc.vector.quantize_mx(
+            out=oq_w[:].bitcast(FP8X4), scales=oq_s[:], in_=res_bf[:].rearrange("p j t -> p (j t)")
+        )
+        nc.sync.dma_start(out=words_of(out_1), in_=oq_w[:].bitcast(I32))
+        for q in range(QUADS):
+            queue = nc.scalar if q % 2 == 0 else nc.sync
+            queue.dma_start(
+                out=out_2[0, 4 * q : 4 * q + 4, :].bitcast(I32),
+                in_=oq_s[32 * q : 32 * q + 4, :].bitcast(I32),
+            )

@@ -73,6 +73,10 @@ def tile_picked_mixinliftharm_none_po_kernel(
         nc.sync.dma_start(offs_t[:], offs)
         nc.scalar.dma_start(out=w1w[:].bitcast(I32), in_=words_of(w1_words))
         nc.scalar.dma_start(out=xw[:].bitcast(I32), in_=words_of(x_words))
+        warm_in = sb([P, 1], F32, "warm_in")
+        warm_out = sb([P, 1], F32, "warm_out")
+        nc.gpsimd.memset(warm_in[:], 1.0)
+        nc.scalar.activation(out=warm_out[:], in_=warm_in[:], func=ACT.Abs_reciprocal_sqrt)
         load_scale_rows(nc.sync, xs, 0, x_scales)
         nc.sync.dma_start(n1_t[:], n1)
         nc.sync.dma_start(n2_t[:], n2)

@@ -18,15 +18,16 @@ ACT = mybir.ActivationFunctionType
 P = 128
 PACK = 4
 QUADS = 4
+SPLIT = 2
 
 
 def words_of(dram):
     return dram[0].rearrange("p n t -> p (n t)").bitcast(I32)
 
 
-def load_scale_rows(queue, tile, first, dram):
+def load_scale_rows(queues, tile, first, dram):
     for q in range(QUADS):
-        queue.dma_start(
+        queues[q].dma_start(
             out=tile[32 * q + first : 32 * q + first + 4, :].bitcast(I32),
             in_=dram[0, 4 * q : 4 * q + 4, :].bitcast(I32),
         )
@@ -66,27 +67,27 @@ def tile_picked_mixinliftharm_none_po_kernel(
         w23s = sb([P, N], U8, "w23s")
         gn_t = sb([P, PACK], F32, "gn_t")
 
+        warm_in = sb([P, 1], F32, "warm_in")
+        warm_out = sb([P, 1], F32, "warm_out")
         nc.vector.memset(xs[:].bitcast(I32), 0)
-        nc.vector.memset(w1s[:].bitcast(I32), 0)
+        nc.gpsimd.memset(w1s[:].bitcast(I32), 0)
+        nc.gpsimd.memset(warm_in[:], 1.0)
         nc.gpsimd.memset(w23s[:].bitcast(I32), 0)
 
         nc.sync.dma_start(offs_t[:], offs)
         nc.scalar.dma_start(out=w1w[:].bitcast(I32), in_=words_of(w1_words))
         nc.scalar.dma_start(out=xw[:].bitcast(I32), in_=words_of(x_words))
-        warm_in = sb([P, 1], F32, "warm_in")
-        warm_out = sb([P, 1], F32, "warm_out")
-        nc.gpsimd.memset(warm_in[:], 1.0)
         nc.scalar.activation(out=warm_out[:], in_=warm_in[:], func=ACT.Abs_reciprocal_sqrt)
-        load_scale_rows(nc.sync, xs, 0, x_scales)
+        load_scale_rows([nc.sync] * 4, xs, 0, x_scales)
+        load_scale_rows([nc.sync] * 3 + [nc.gpsimd], w1s, 0, w1_scales)
         nc.sync.dma_start(n1_t[:], n1)
         nc.sync.dma_start(n2_t[:], n2)
-        load_scale_rows(nc.scalar, w1s, 0, w1_scales)
         nc.sync.dma_start(two_t[:], two)
         nc.sync.dma_start(out=gn_t[:], in_=gn.rearrange("(p t) o -> p (t o)", t=PACK))
         nc.sync.dma_start(out=w3w[:].bitcast(I32), in_=words_of(w3_words))
+        load_scale_rows([nc.sync] * 4, w23s, 0, w3_scales)
+        load_scale_rows([nc.sync] * 4, w23s, 4, w2_scales)
         nc.sync.dma_start(out=w2w[:].bitcast(I32), in_=words_of(w2_words))
-        load_scale_rows(nc.sync, w23s, 0, w3_scales)
-        load_scale_rows(nc.sync, w23s, 4, w2_scales)
         nc.sync.dma_start(n3_t[:], n3)
 
         w1w_d = sb([P, H], U32, "w1w_d")
@@ -96,7 +97,8 @@ def tile_picked_mixinliftharm_none_po_kernel(
         nc.vector.tensor_copy(out=xq_s[:], in_=xs[:].indirect(offs_t[:]))
         xq_w = sb([P, S], U32, "xq_w")
         nc.vector.tensor_copy(out=xq_w[:], in_=xw[:].indirect(offs_t[:]))
-        nc.vector.tensor_copy(out=dealt(w1s_d[:]), in_=plain(w1s[:]))
+        nc.vector.tensor_copy(out=w1s_d[:, 0:P], in_=plain(w1s[:])[:, :, 0])
+        nc.vector.tensor_copy(out=dealt(w1s_d[:])[:, :, 1:PACK], in_=plain(w1s[:])[:, :, 1:PACK])
 
         y = []
         for t in range(PACK):
@@ -112,29 +114,32 @@ def tile_picked_mixinliftharm_none_po_kernel(
 
         pa = [sb([P, W], F32, f"pa{t}") for t in range(PACK)]
         pb = [sb([P, W], F32, f"pb{t}") for t in range(PACK)]
-        ra = [sb([P, W], F32, f"ra{t}") for t in range(PACK)]
-        rb = [sb([P, W], F32, f"rb{t}") for t in range(PACK)]
+        wide = [sb([P, 2 * S], F32, f"wide{t}") for t in range(PACK)]
+        ra = [wide[t][:, S : S + W] for t in range(PACK)]
+        rb = [wide[t][:, S + W : 2 * S] for t in range(PACK)]
         dt = [sb([P, S], F32, f"dt{t}") for t in range(PACK)]
-        z = sb([P, S, PACK], BF16, "z")
+        z = [sb([P, W, PACK], BF16, f"z{u}") for u in range(2)]
 
         def fetch_a(t):
             nc.scalar.activation(out=pa[t][:], in_=y[t][:].indirect(n1_t[:]), func=ACT.Copy)
 
         def fetch_b(t):
             nc.scalar.activation(out=pb[t][:], in_=y[t][:].indirect(n2_t[:]), func=ACT.Copy)
-            nc.vector.tensor_tensor(out=ra[t][:], in0=pb[t][:], in1=pa[t][:], op=ALU.subtract)
+            nc.vector.tensor_tensor(out=ra[t], in0=pb[t][:], in1=pa[t][:], op=ALU.subtract)
             nc.vector.scalar_tensor_tensor(
-                out=rb[t][:], in0=pa[t][:], scalar=0.5, in1=pb[t][:], op0=ALU.mult, op1=ALU.max
+                out=rb[t], in0=pa[t][:], scalar=0.5, in1=pb[t][:], op0=ALU.mult, op1=ALU.max
             )
 
         def put_a(t):
-            nc.scalar.activation(out=dt[t][:].indirect(n1_t[:]), in_=ra[t][:], func=ACT.Copy)
+            nc.scalar.activation(out=dt[t][:].indirect(n1_t[:]), in_=ra[t], func=ACT.Copy)
 
         def put_b(t):
-            nc.scalar.activation(out=dt[t][:].indirect(n2_t[:]), in_=rb[t][:], func=ACT.Copy)
-            nc.vector.tensor_scalar(
-                out=z[:, :, t], in0=dt[t][:], scalar1=gn_t[:, t : t + 1], scalar2=None, op0=ALU.mult
-            )
+            nc.scalar.activation(out=dt[t][:].indirect(n2_t[:]), in_=rb[t], func=ACT.Copy)
+            for u in range(2):
+                nc.vector.tensor_scalar(
+                    out=z[u][:, :, t], in0=dt[t][:, u * W : (u + 1) * W],
+                    scalar1=gn_t[:, t : t + 1], scalar2=None, op0=ALU.mult,
+                )
 
         fetch_a(0)
         fetch_b(0)
@@ -143,7 +148,6 @@ def tile_picked_mixinliftharm_none_po_kernel(
 
         w3w_d = sb([P, N], U32, "w3w_d")
         w2w_d = sb([P, N], U32, "w2w_d")
-        w23s_d = sb([P, N], U8, "w23s_d")
         x2_w = sb([P, S], U32, "x2_w")
         x2_s = sb([P, S], U8, "x2_s")
 
@@ -157,9 +161,12 @@ def tile_picked_mixinliftharm_none_po_kernel(
         fetch_a(3)
         put_b(1)
         fetch_b(3)
-        nc.vector.tensor_copy(out=dealt(w3w_d[:]), in_=plain(w3w[:]))
-        nc.gpsimd.tensor_copy(out=dealt(w23s_d[:]), in_=plain(w23s[:]))
-        nc.vector.tensor_copy(out=dealt(w2w_d[:]), in_=plain(w2w[:]))
+        w23s_d = sb([P, N], U8, "w23s_d")
+        for moved, loaded in ((w3w_d, w3w), (w23s_d, w23s), (w2w_d, w2w)):
+            nc.gpsimd.tensor_copy(
+                out=moved[:].rearrange("p (t m) -> p t m", t=PACK),
+                in_=loaded[:].rearrange("p (m t) -> p t m", t=PACK),
+            )
         h_ps = [psum.tile([P, S], F32, name=f"h_ps{t}") for t in range(PACK)]
         for t in range(PACK):
             cols = slice(t * P, (t + 1) * P)
@@ -174,93 +181,88 @@ def tile_picked_mixinliftharm_none_po_kernel(
 
         zq_w = sb([P, S], U32, "zq_w")
         zq_s = sb([P, S], U8, "zq_s")
-        nc.vector.quantize_mx(
-            out=zq_w[:].bitcast(FP8X4), scales=zq_s[:], in_=z[:].rearrange("p j t -> p (j t)")
-        )
+        halves = [slice(u * W, (u + 1) * W) for u in range(2)]
+        for u in range(2):
+            nc.vector.quantize_mx(
+                out=zq_w[:, halves[u]].bitcast(FP8X4), scales=zq_s[:, halves[u]],
+                in_=z[u][:].rearrange("p j t -> p (j t)"),
+            )
         for t in range(PACK):
             cols = slice(t * P, (t + 1) * P)
-            nc.tensor.matmul_mx(
-                out=h_ps[t][:], lhsT=w2w_d[:, cols].bitcast(FP8X4), lhsT_scale=w23s_d[4:P, cols],
-                rhs=zq_w[:].bitcast(FP8X4), rhs_scale=zq_s[:], start=False, stop=True,
-            )
+            for u in range(2):
+                nc.tensor.matmul_mx(
+                    out=h_ps[t][:, halves[u]], lhsT=w2w_d[:, cols].bitcast(FP8X4), lhsT_scale=w23s_d[4:P, cols],
+                    rhs=zq_w[:, halves[u]].bitcast(FP8X4), rhs_scale=zq_s[:, halves[u]], start=False, stop=(u == 1),
+                )
 
-        h = [sb([P, S], F32, f"h{t}") for t in range(PACK)]
+        h = [wide[t][:, 0:S] for t in range(PACK)]
         pa2 = [sb([P, S], F32, f"pa2_{t}") for t in range(PACK)]
         hh = [sb([P, S], F32, f"hh{t}") for t in range(PACK)]
         pp = [sb([P, S], F32, f"pp{t}") for t in range(PACK)]
         den = [sb([P, S], F32, f"den{t}") for t in range(PACK)]
         rs = [sb([P, S], F32, f"rs{t}") for t in range(PACK)]
         num = [sb([P, S], F32, f"num{t}") for t in range(PACK)]
-        half = [sb([P, S], F32, f"half{t}") for t in range(PACK)]
+        mid = [sb([P, S], F32, f"mid{t}") for t in range(PACK)]
         res = [sb([P, 2, S], F32, f"res{u}") for u in range(2)]
-        res_bf = sb([P, S, PACK], BF16, "res_bf")
-        out_rows = out_0.rearrange("(p t) j -> p t j", t=PACK)
-
-        def leave(t, on_scalar):
-            if on_scalar:
-                nc.scalar.copy(out=h[t][:], in_=h_ps[t][:])
-            else:
-                nc.vector.tensor_copy(out=h[t][:], in_=h_ps[t][:])
-
-        def fetch(t):
-            for u in range(2):
-                nc.scalar.activation(
-                    out=pa2[t][:, u * W : (u + 1) * W],
-                    in_=h[t][:].indirect(n3_t[:, u * 8 : (u + 1) * 8]), func=ACT.Copy,
-                )
-
-        def square_h(t, on_scalar):
-            if on_scalar:
-                nc.scalar.activation(out=hh[t][:], in_=h[t][:], func=ACT.Square)
-            else:
-                nc.vector.tensor_tensor(out=hh[t][:], in0=h[t][:], in1=h[t][:], op=ALU.mult)
-
-        def sums(t):
-            nc.scalar.activation(out=pp[t][:], in_=pa2[t][:], func=ACT.Square)
-            nc.vector.scalar_tensor_tensor(
-                out=num[t][:], in0=h[t][:], scalar=2.0, in1=pa2[t][:], op0=ALU.mult, op1=ALU.mult
-            )
-            nc.vector.scalar_tensor_tensor(
-                out=den[t][:], in0=hh[t][:], scalar=0.5, in1=pp[t][:], op0=ALU.add, op1=ALU.add
-            )
-
-        def finish(t):
-            nc.scalar.activation(out=rs[t][:], in_=den[t][:], func=ACT.Abs_reciprocal_sqrt)
-            nc.vector.tensor_tensor(out=half[t][:], in0=num[t][:], in1=rs[t][:], op=ALU.mult)
-            nc.vector.tensor_tensor(out=res[t // 2][:, t % 2, :], in0=half[t][:], in1=rs[t][:], op=ALU.mult)
-            nc.sync.dma_start(out=out_rows[:, t, :], in_=res[t // 2][:, t % 2, :])
-            if t % 2 == 1:
-                nc.vector.tensor_copy(
-                    out=res_bf[:, :, t - 1 : t + 1], in_=res[t // 2][:].rearrange("p t j -> p j t")
-                )
-
-        leave(0, False)
-        leave(1, True)
-        leave(2, False)
-        leave(3, False)
-        fetch(0)
-        square_h(0, False)
-        square_h(1, False)
-        sums(0)
-        fetch(1)
-        finish(0)
-        sums(1)
-        fetch(2)
-        square_h(2, True)
-        finish(1)
-        sums(2)
-        fetch(3)
-        square_h(3, True)
-        sums(3)
-        finish(2)
-        finish(3)
-
+        res_bf = [sb([P, W, PACK], BF16, f"res_bf{u}") for u in range(2)]
         oq_w = sb([P, S], U32, "oq_w")
         oq_s = sb([P, S], U8, "oq_s")
-        nc.vector.quantize_mx(
-            out=oq_w[:].bitcast(FP8X4), scales=oq_s[:], in_=res_bf[:].rearrange("p j t -> p (j t)")
-        )
-        nc.sync.dma_start(out=words_of(out_1), in_=oq_w[:].bitcast(I32))
+        out_rows = out_0.rearrange("(p t) j -> p t j", t=PACK)
+        out_words = words_of(out_1)
+
+        def square(out, in_, on_vector):
+            if on_vector:
+                nc.vector.tensor_tensor(out=out, in0=in_, in1=in_, op=ALU.mult)
+            else:
+                nc.scalar.activation(out=out, in_=in_, func=ACT.Square)
+
+        def pieces(t):
+            return [slice(0, S)] if t < SPLIT else halves
+
+        def front(t):
+            square(hh[t][:], h[t], t < 2)
+            for c in pieces(t):
+                square(pp[t][:, c], pa2[t][:, c], t < 2)
+                nc.vector.scalar_tensor_tensor(
+                    out=den[t][:, c], in0=hh[t][:, c], scalar=0.5, in1=pp[t][:, c], op0=ALU.add, op1=ALU.add
+                )
+                nc.vector.scalar_tensor_tensor(
+                    out=num[t][:, c], in0=h[t][:, c], scalar=2.0, in1=pa2[t][:, c], op0=ALU.mult, op1=ALU.mult
+                )
+
+        def back(t):
+            for c in pieces(t):
+                nc.scalar.activation(out=rs[t][:, c], in_=den[t][:, c], func=ACT.Abs_reciprocal_sqrt)
+                if t < 2:
+                    nc.vector.tensor_tensor(out=mid[t][:, c], in0=num[t][:, c], in1=rs[t][:, c], op=ALU.mult)
+                    nc.vector.tensor_tensor(
+                        out=res[t // 2][:, t % 2, c], in0=mid[t][:, c], in1=rs[t][:, c], op=ALU.mult
+                    )
+                else:
+                    nc.scalar.activation(out=mid[t][:, c], in_=rs[t][:, c], func=ACT.Square)
+                    nc.vector.tensor_tensor(
+                        out=res[t // 2][:, t % 2, c], in0=num[t][:, c], in1=mid[t][:, c], op=ALU.mult
+                    )
+            nc.sync.dma_start(out=out_rows[:, t, :], in_=res[t // 2][:, t % 2, :])
+
+        for t in range(PACK):
+            nc.vector.tensor_copy(out=h[t], in_=h_ps[t][:])
+        for t in range(PACK):
+            nc.scalar.activation(out=pa2[t][:], in_=wide[t][:].indirect(n3_t[:]), func=ACT.Copy)
+        for t in range(PACK):
+            front(t)
+        for t in range(PACK):
+            back(t)
+        for u in range(2):
+            nc.scalar.copy(out=res_bf[u][:, :, 0:2], in_=res[0][:, :, halves[u]].rearrange("p t j -> p j t"))
+        for u in range(2):
+            nc.vector.tensor_copy(out=res_bf[u][:, :, 2:4], in_=res[1][:, :, halves[u]].rearrange("p t j -> p j t"))
+        for u in range(2):
+            nc.vector.quantize_mx(
+                out=oq_w[:, halves[u]].bitcast(FP8X4), scales=oq_s[:, halves[u]],
+                in_=res_bf[u][:].rearrange("p j t -> p (j t)"),
+            )
+            nc.sync.dma_start(out=out_words[:, halves[u]], in_=oq_w[:, halves[u]].bitcast(I32))
         for q in range(QUADS):
             queue = nc.scalar if q % 2 == 0 else nc.sync
             queue.dma_start(

@@ -19,15 +19,16 @@ P = 128
 PACK = 4
 QUADS = 4
 SPLIT = 2
+XS_SPLIT = 320
 
 
 def words_of(dram):
     return dram[0].rearrange("p n t -> p (n t)").bitcast(I32)
 
 
-def load_scale_rows(queues, tile, first, dram):
-    for q in range(QUADS):
-        queues[q].dma_start(
+def load_scale_rows(queue, quads, tile, first, dram):
+    for q in quads:
+        queue.dma_start(
             out=tile[32 * q + first : 32 * q + first + 4, :].bitcast(I32),
             in_=dram[0, 4 * q : 4 * q + 4, :].bitcast(I32),
         )
@@ -69,25 +70,28 @@ def tile_picked_mixinliftharm_none_po_kernel(
 
         warm_in = sb([P, 1], F32, "warm_in")
         warm_out = sb([P, 1], F32, "warm_out")
-        nc.vector.memset(xs[:].bitcast(I32), 0)
+        xs_words = xs[:].bitcast(I32)
+        nc.vector.memset(xs_words[:, 0:XS_SPLIT], 0)
+        nc.gpsimd.memset(xs_words[:, XS_SPLIT : T // 4], 0)
         nc.gpsimd.memset(w1s[:].bitcast(I32), 0)
-        nc.gpsimd.memset(warm_in[:], 1.0)
-        nc.gpsimd.memset(w23s[:].bitcast(I32), 0)
+        nc.vector.memset(warm_in[:], 1.0)
+        nc.vector.memset(w23s[:].bitcast(I32), 0)
 
         nc.sync.dma_start(offs_t[:], offs)
         nc.scalar.dma_start(out=w1w[:].bitcast(I32), in_=words_of(w1_words))
+        load_scale_rows(nc.sync, range(QUADS), xs, 0, x_scales)
         nc.scalar.dma_start(out=xw[:].bitcast(I32), in_=words_of(x_words))
         nc.scalar.activation(out=warm_out[:], in_=warm_in[:], func=ACT.Abs_reciprocal_sqrt)
-        load_scale_rows([nc.sync] * 4, xs, 0, x_scales)
-        load_scale_rows([nc.sync] * 3 + [nc.gpsimd], w1s, 0, w1_scales)
+        load_scale_rows(nc.sync, [0, 1, 2], w1s, 0, w1_scales)
+        load_scale_rows(nc.gpsimd, [3], w1s, 0, w1_scales)
         nc.sync.dma_start(n1_t[:], n1)
         nc.sync.dma_start(n2_t[:], n2)
-        nc.sync.dma_start(two_t[:], two)
-        nc.sync.dma_start(out=gn_t[:], in_=gn.rearrange("(p t) o -> p (t o)", t=PACK))
         nc.sync.dma_start(out=w3w[:].bitcast(I32), in_=words_of(w3_words))
-        load_scale_rows([nc.sync] * 4, w23s, 0, w3_scales)
-        load_scale_rows([nc.sync] * 4, w23s, 4, w2_scales)
         nc.sync.dma_start(out=w2w[:].bitcast(I32), in_=words_of(w2_words))
+        nc.sync.dma_start(two_t[:], two)
+        load_scale_rows(nc.sync, range(QUADS), w23s, 0, w3_scales)
+        load_scale_rows(nc.sync, range(QUADS), w23s, 4, w2_scales)
+        nc.sync.dma_start(out=gn_t[:], in_=gn.rearrange("(p t) o -> p (t o)", t=PACK))
         nc.sync.dma_start(n3_t[:], n3)
 
         w1w_d = sb([P, H], U32, "w1w_d")
@@ -97,7 +101,7 @@ def tile_picked_mixinliftharm_none_po_kernel(
         nc.vector.tensor_copy(out=xq_s[:], in_=xs[:].indirect(offs_t[:]))
         xq_w = sb([P, S], U32, "xq_w")
         nc.vector.tensor_copy(out=xq_w[:], in_=xw[:].indirect(offs_t[:]))
-        nc.vector.tensor_copy(out=w1s_d[:, 0:P], in_=plain(w1s[:])[:, :, 0])
+        nc.gpsimd.tensor_copy(out=w1s_d[:, 0:P], in_=plain(w1s[:])[:, :, 0])
         nc.vector.tensor_copy(out=dealt(w1s_d[:])[:, :, 1:PACK], in_=plain(w1s[:])[:, :, 1:PACK])
 
         y = []
@@ -162,11 +166,8 @@ def tile_picked_mixinliftharm_none_po_kernel(
         put_b(1)
         fetch_b(3)
         w23s_d = sb([P, N], U8, "w23s_d")
-        for moved, loaded in ((w3w_d, w3w), (w23s_d, w23s), (w2w_d, w2w)):
-            nc.gpsimd.tensor_copy(
-                out=moved[:].rearrange("p (t m) -> p t m", t=PACK),
-                in_=loaded[:].rearrange("p (m t) -> p t m", t=PACK),
-            )
+        for moved, loaded in ((w3w_d, w3w), (w2w_d, w2w), (w23s_d, w23s)):
+            nc.vector.tensor_copy(out=dealt(moved[:]), in_=plain(loaded[:]))
         h_ps = [psum.tile([P, S], F32, name=f"h_ps{t}") for t in range(PACK)]
         for t in range(PACK):
             cols = slice(t * P, (t + 1) * P)

@@ -78,12 +78,12 @@ def tile_picked_mixinliftharm_none_po_kernel(
         nc.vector.memset(w23s[:].bitcast(I32), 0)
 
         nc.sync.dma_start(offs_t[:], offs)
-        nc.scalar.dma_start(out=w1w[:].bitcast(I32), in_=words_of(w1_words))
-        load_scale_rows(nc.sync, range(QUADS), xs, 0, x_scales)
-        nc.scalar.dma_start(out=xw[:].bitcast(I32), in_=words_of(x_words))
+        load_scale_rows(nc.sync, [0, 1], xs, 0, x_scales)
+        load_scale_rows(nc.scalar, [2, 3], xs, 0, x_scales)
+        load_scale_rows(nc.scalar, range(QUADS), w1s, 0, w1_scales)
         nc.scalar.activation(out=warm_out[:], in_=warm_in[:], func=ACT.Abs_reciprocal_sqrt)
-        load_scale_rows(nc.sync, [0, 1, 2], w1s, 0, w1_scales)
-        load_scale_rows(nc.gpsimd, [3], w1s, 0, w1_scales)
+        nc.sync.dma_start(out=xw[:].bitcast(I32), in_=words_of(x_words))
+        nc.sync.dma_start(out=w1w[:].bitcast(I32), in_=words_of(w1_words))
         nc.sync.dma_start(n1_t[:], n1)
         nc.sync.dma_start(n2_t[:], n2)
         nc.sync.dma_start(out=w3w[:].bitcast(I32), in_=words_of(w3_words))
@@ -94,22 +94,26 @@ def tile_picked_mixinliftharm_none_po_kernel(
         nc.sync.dma_start(out=gn_t[:], in_=gn.rearrange("(p t) o -> p (t o)", t=PACK))
         nc.sync.dma_start(n3_t[:], n3)
 
-        w1w_d = sb([P, H], U32, "w1w_d")
-        w1s_d = sb([P, H], U8, "w1s_d")
-        nc.vector.tensor_copy(out=dealt(w1w_d[:]), in_=plain(w1w[:]))
         xq_s = sb([P, S], U8, "xq_s")
         nc.vector.tensor_copy(out=xq_s[:], in_=xs[:].indirect(offs_t[:]))
         xq_w = sb([P, S], U32, "xq_w")
         nc.vector.tensor_copy(out=xq_w[:], in_=xw[:].indirect(offs_t[:]))
-        nc.gpsimd.tensor_copy(out=w1s_d[:, 0:P], in_=plain(w1s[:])[:, :, 0])
-        nc.vector.tensor_copy(out=dealt(w1s_d[:])[:, :, 1:PACK], in_=plain(w1s[:])[:, :, 1:PACK])
+        w1s_d = [sb([P, P], U8, f"w1s_d{t}") for t in range(PACK)]
+        for t in range(PACK):
+            nc.gpsimd.tensor_copy(out=w1s_d[t][:], in_=plain(w1s[:])[:, :, t])
+        w1w_first = sb([P, P], U32, "w1w_first")
+        w1w_rest = sb([P, H - P], U32, "w1w_rest")
+        nc.scalar.copy(out=w1w_first[:], in_=plain(w1w[:])[:, :, 0])
+        nc.vector.tensor_copy(
+            out=w1w_rest[:].rearrange("p (t m) -> p m t", m=P), in_=plain(w1w[:])[:, :, 1:PACK]
+        )
+        w1w_d = [w1w_first[:]] + [w1w_rest[:, (t - 1) * P : t * P] for t in range(1, PACK)]
 
         y = []
         for t in range(PACK):
-            cols = slice(t * P, (t + 1) * P)
             y_ps = psum.tile([P, S], F32, name=f"y_ps{t}")
             nc.tensor.matmul_mx(
-                out=y_ps[:], lhsT=w1w_d[:, cols].bitcast(FP8X4), lhsT_scale=w1s_d[:, cols],
+                out=y_ps[:], lhsT=w1w_d[t].bitcast(FP8X4), lhsT_scale=w1s_d[t][:],
                 rhs=xq_w[:].bitcast(FP8X4), rhs_scale=xq_s[:], start=True, stop=True,
             )
             y_t = sb([P, S], F32, f"y{t}")

from contextlib import ExitStack

import concourse.mybir as mybir

K, T, S, N, H, W = 512, 2048, 256, 512, 512, 128
FLOPS = 3 * 2 * 512 * 512 * 256

F32 = mybir.dt.float32
BF16 = mybir.dt.bfloat16
I32 = mybir.dt.int32
U32 = mybir.dt.uint32
U16 = mybir.dt.uint16
U8 = mybir.dt.uint8
FP8X4 = mybir.dt.float8_e4m3fn_x4
ALU = mybir.AluOpType
ACT = mybir.ActivationFunctionType

P = 128
PACK = 4
QUADS = 4
SPLIT = 2
XS_SPLIT = 320


def words_of(dram):
    return dram[0].rearrange("p n t -> p (n t)").bitcast(I32)


def load_scale_rows(queue, quads, tile, first, dram):
    for q in quads:
        queue.dma_start(
            out=tile[32 * q + first : 32 * q + first + 4, :].bitcast(I32),
            in_=dram[0, 4 * q : 4 * q + 4, :].bitcast(I32),
        )


def dealt(ap):
    return ap.rearrange("p (t m) -> p m t", t=PACK)


def plain(ap):
    return ap.rearrange("p (m t) -> p m t", t=PACK)


def tile_picked_mixinliftharm_none_po_kernel(
    tc, x_words, x_scales, w1_words, w1_scales, gn, w2_words, w2_scales, w3_words, w3_scales,
    offs, n1, n2, two, n3, out_0, out_1, out_2,
):
    nc = tc.nc
    with ExitStack() as ctx:
        keep = ctx.enter_context(tc.tile_pool(name="keep", bufs=1))
        psum = ctx.enter_context(tc.psum_pool(name="psum", bufs=1))

        def sb(shape, dtype, name):
            return keep.tile(shape, dtype, name=name, align_bytes=64)

        offs_t = sb([P, S // 16], U16, "offs_t")
        n1_t = sb([P, W // 16], U16, "n1_t")
        n2_t = sb([P, W // 16], U16, "n2_t")
        two_t = sb([P, S // 16], U16, "two_t")
        n3_t = sb([P, S // 16], U16, "n3_t")
        xw = sb([P, T], U32, "xw")
        xs = sb([P, T], U8, "xs")
        w1w = sb([P, H], U32, "w1w")
        w2w = sb([P, N], U32, "w2w")
        w3w = sb([P, N], U32, "w3w")
        w1s = sb([P, H], U8, "w1s")
        w23s = sb([P, N], U8, "w23s")
        gn_t = sb([P, PACK], F32, "gn_t")

        warm_in = sb([P, 1], F32, "warm_in")
        warm_out = sb([P, 1], F32, "warm_out")
        xs_words = xs[:].bitcast(I32)
        nc.vector.memset(xs_words[:, 0:XS_SPLIT], 0)
        nc.gpsimd.memset(xs_words[:, XS_SPLIT : T // 4], 0)
        nc.gpsimd.memset(w1s[:].bitcast(I32), 0)
        nc.vector.memset(warm_in[:], 1.0)
        nc.vector.memset(w23s[:].bitcast(I32), 0)

        nc.sync.dma_start(offs_t[:], offs)
        load_scale_rows(nc.sync, [0, 1], xs, 0, x_scales)
        load_scale_rows(nc.scalar, [2, 3], xs, 0, x_scales)
        load_scale_rows(nc.scalar, range(QUADS), w1s, 0, w1_scales)
        nc.scalar.activation(out=warm_out[:], in_=warm_in[:], func=ACT.Abs_reciprocal_sqrt)
        nc.sync.dma_start(out=xw[:].bitcast(I32), in_=words_of(x_words))
        nc.sync.dma_start(out=w1w[:].bitcast(I32), in_=words_of(w1_words))
        nc.sync.dma_start(n1_t[:], n1)
        nc.sync.dma_start(n2_t[:], n2)
        nc.sync.dma_start(out=w3w[:].bitcast(I32), in_=words_of(w3_words))
        nc.sync.dma_start(out=w2w[:].bitcast(I32), in_=words_of(w2_words))
        nc.sync.dma_start(two_t[:], two)
        load_scale_rows(nc.sync, range(QUADS), w23s, 0, w3_scales)
        load_scale_rows(nc.sync, range(QUADS), w23s, 4, w2_scales)
        nc.sync.dma_start(out=gn_t[:], in_=gn.rearrange("(p t) o -> p (t o)", t=PACK))
        nc.sync.dma_start(n3_t[:], n3)

        xq_s = sb([P, S], U8, "xq_s")
        nc.vector.tensor_copy(out=xq_s[:], in_=xs[:].indirect(offs_t[:]))
        xq_w = sb([P, S], U32, "xq_w")
        nc.vector.tensor_copy(out=xq_w[:], in_=xw[:].indirect(offs_t[:]))
        w1s_d = [sb([P, P], U8, f"w1s_d{t}") for t in range(PACK)]
        for t in range(PACK):
            nc.gpsimd.tensor_copy(out=w1s_d[t][:], in_=plain(w1s[:])[:, :, t])
        w1w_first = sb([P, P], U32, "w1w_first")
        w1w_rest = sb([P, H - P], U32, "w1w_rest")
        nc.scalar.copy(out=w1w_first[:], in_=plain(w1w[:])[:, :, 0])
        nc.vector.tensor_copy(
            out=w1w_rest[:].rearrange("p (t m) -> p m t", m=P), in_=plain(w1w[:])[:, :, 1:PACK]
        )
        w1w_d = [w1w_first[:]] + [w1w_rest[:, (t - 1) * P : t * P] for t in range(1, PACK)]

        y = []
        for t in range(PACK):
            y_ps = psum.tile([P, S], F32, name=f"y_ps{t}")
            nc.tensor.matmul_mx(
                out=y_ps[:], lhsT=w1w_d[t].bitcast(FP8X4), lhsT_scale=w1s_d[t][:],
                rhs=xq_w[:].bitcast(FP8X4), rhs_scale=xq_s[:], start=True, stop=True,
            )
            y_t = sb([P, S], F32, f"y{t}")
            nc.vector.tensor_copy(out=y_t[:], in_=y_ps[:])
            y.append(y_t)

        pa = [sb([P, W], F32, f"pa{t}") for t in range(PACK)]
        pb = [sb([P, W], F32, f"pb{t}") for t in range(PACK)]
        wide = [sb([P, 2 * S], F32, f"wide{t}") for t in range(PACK)]
        ra = [wide[t][:, S : S + W] for t in range(PACK)]
        rb = [wide[t][:, S + W : 2 * S] for t in range(PACK)]
        dt = [sb([P, S], F32, f"dt{t}") for t in range(PACK)]
        z = [sb([P, W, PACK], BF16, f"z{u}") for u in range(2)]

        def fetch_a(t):
            nc.scalar.activation(out=pa[t][:], in_=y[t][:].indirect(n1_t[:]), func=ACT.Copy)

        def fetch_b(t):
            nc.scalar.activation(out=pb[t][:], in_=y[t][:].indirect(n2_t[:]), func=ACT.Copy)
            nc.vector.tensor_tensor(out=ra[t], in0=pb[t][:], in1=pa[t][:], op=ALU.subtract)
            nc.vector.scalar_tensor_tensor(
                out=rb[t], in0=pa[t][:], scalar=0.5, in1=pb[t][:], op0=ALU.mult, op1=ALU.max
            )

        def put_a(t):
            nc.scalar.activation(out=dt[t][:].indirect(n1_t[:]), in_=ra[t], func=ACT.Copy)

        def put_b(t):
            nc.scalar.activation(out=dt[t][:].indirect(n2_t[:]), in_=rb[t], func=ACT.Copy)
            for u in range(2):
                nc.vector.tensor_scalar(
                    out=z[u][:, :, t], in0=dt[t][:, u * W : (u + 1) * W],
                    scalar1=gn_t[:, t : t + 1], scalar2=None, op0=ALU.mult,
                )

        fetch_a(0)
        fetch_b(0)
        fetch_a(1)
        fetch_b(1)

        w3w_d = sb([P, N], U32, "w3w_d")
        w2w_d = sb([P, N], U32, "w2w_d")
        x2_w = sb([P, S], U32, "x2_w")
        x2_s = sb([P, S], U8, "x2_s")

        put_a(0)
        fetch_a(2)
        put_b(0)
        fetch_b(2)
        nc.vector.tensor_copy(out=x2_w[:], in_=xw[:].indirect(two_t[:]))
        nc.vector.tensor_copy(out=x2_s[:], in_=xs[:].indirect(two_t[:]))
        put_a(1)
        fetch_a(3)
        put_b(1)
        fetch_b(3)
        w23s_d = sb([P, N], U8, "w23s_d")
        for moved, loaded in ((w3w_d, w3w), (w2w_d, w2w), (w23s_d, w23s)):
            nc.vector.tensor_copy(out=dealt(moved[:]), in_=plain(loaded[:]))
        h_ps = [psum.tile([P, S], F32, name=f"h_ps{t}") for t in range(PACK)]
        for t in range(PACK):
            cols = slice(t * P, (t + 1) * P)
            nc.tensor.matmul_mx(
                out=h_ps[t][:], lhsT=w3w_d[:, cols].bitcast(FP8X4), lhsT_scale=w23s_d[:, cols],
                rhs=x2_w[:].bitcast(FP8X4), rhs_scale=x2_s[:], start=True, stop=False,
            )
        put_a(2)
        put_a(3)
        put_b(2)
        put_b(3)

        zq_w = sb([P, S], U32, "zq_w")
        zq_s = sb([P, S], U8, "zq_s")
        halves = [slice(u * W, (u + 1) * W) for u in range(2)]
        for u in range(2):
            nc.vector.quantize_mx(
                out=zq_w[:, halves[u]].bitcast(FP8X4), scales=zq_s[:, halves[u]],
                in_=z[u][:].rearrange("p j t -> p (j t)"),
            )
        for t in range(PACK):
            cols = slice(t * P, (t + 1) * P)
            for u in range(2):
                nc.tensor.matmul_mx(
                    out=h_ps[t][:, halves[u]], lhsT=w2w_d[:, cols].bitcast(FP8X4), lhsT_scale=w23s_d[4:P, cols],
                    rhs=zq_w[:, halves[u]].bitcast(FP8X4), rhs_scale=zq_s[:, halves[u]], start=False, stop=(u == 1),
                )

        h = [wide[t][:, 0:S] for t in range(PACK)]
        pa2 = [sb([P, S], F32, f"pa2_{t}") for t in range(PACK)]
        hh = [sb([P, S], F32, f"hh{t}") for t in range(PACK)]
        pp = [sb([P, S], F32, f"pp{t}") for t in range(PACK)]
        den = [sb([P, S], F32, f"den{t}") for t in range(PACK)]
        rs = [sb([P, S], F32, f"rs{t}") for t in range(PACK)]
        num = [sb([P, S], F32, f"num{t}") for t in range(PACK)]
        mid = [sb([P, S], F32, f"mid{t}") for t in range(PACK)]
        res = [sb([P, 2, S], F32, f"res{u}") for u in range(2)]
        res_bf = [sb([P, W, PACK], BF16, f"res_bf{u}") for u in range(2)]
        oq_w = sb([P, S], U32, "oq_w")
        oq_s = sb([P, S], U8, "oq_s")
        out_rows = out_0.rearrange("(p t) j -> p t j", t=PACK)
        out_words = words_of(out_1)

        def square(out, in_, on_vector):
            if on_vector:
                nc.vector.tensor_tensor(out=out, in0=in_, in1=in_, op=ALU.mult)
            else:
                nc.scalar.activation(out=out, in_=in_, func=ACT.Square)

        def pieces(t):
            return [slice(0, S)] if t < SPLIT else halves

        def front(t):
            square(hh[t][:], h[t], t < 2)
            for c in pieces(t):
                square(pp[t][:, c], pa2[t][:, c], t < 2)
                nc.vector.scalar_tensor_tensor(
                    out=den[t][:, c], in0=hh[t][:, c], scalar=0.5, in1=pp[t][:, c], op0=ALU.add, op1=ALU.add
                )
                nc.vector.scalar_tensor_tensor(
                    out=num[t][:, c], in0=h[t][:, c], scalar=2.0, in1=pa2[t][:, c], op0=ALU.mult, op1=ALU.mult
                )

        def back(t):
            for c in pieces(t):
                nc.scalar.activation(out=rs[t][:, c], in_=den[t][:, c], func=ACT.Abs_reciprocal_sqrt)
                if t < 2:
                    nc.vector.tensor_tensor(out=mid[t][:, c], in0=num[t][:, c], in1=rs[t][:, c], op=ALU.mult)
                    nc.vector.tensor_tensor(
                        out=res[t // 2][:, t % 2, c], in0=mid[t][:, c], in1=rs[t][:, c], op=ALU.mult
                    )
                else:
                    nc.scalar.activation(out=mid[t][:, c], in_=rs[t][:, c], func=ACT.Square)
                    nc.vector.tensor_tensor(
                        out=res[t // 2][:, t % 2, c], in0=num[t][:, c], in1=mid[t][:, c], op=ALU.mult
                    )
            nc.sync.dma_start(out=out_rows[:, t, :], in_=res[t // 2][:, t % 2, :])

        for t in range(PACK):
            nc.vector.tensor_copy(out=h[t], in_=h_ps[t][:])
        for t in range(PACK):
            nc.scalar.activation(out=pa2[t][:], in_=wide[t][:].indirect(n3_t[:]), func=ACT.Copy)
        for t in range(PACK):
            front(t)
        for t in range(PACK):
            back(t)
        for u in range(2):
            nc.scalar.copy(out=res_bf[u][:, :, 0:2], in_=res[0][:, :, halves[u]].rearrange("p t j -> p j t"))
        for u in range(2):
            nc.vector.tensor_copy(out=res_bf[u][:, :, 2:4], in_=res[1][:, :, halves[u]].rearrange("p t j -> p j t"))
        for u in range(2):
            nc.vector.quantize_mx(
                out=oq_w[:, halves[u]].bitcast(FP8X4), scales=oq_s[:, halves[u]],
                in_=res_bf[u][:].rearrange("p j t -> p (j t)"),
            )
            nc.sync.dma_start(out=out_words[:, halves[u]], in_=oq_w[:, halves[u]].bitcast(I32))
        for q in range(QUADS):
            queue = nc.scalar if q % 2 == 0 else nc.sync
            queue.dma_start(
                out=out_2[0, 4 * q : 4 * q + 4, :].bitcast(I32),
                in_=oq_s[32 * q : 32 * q + 4, :].bitcast(I32),
            )
